import numpy as np
import ml_dtypes


def mxq(x, axis, fmt="e4m3"):
    dtype, down = {"e4m3": (ml_dtypes.float8_e4m3fn, 7), "e5m2": (ml_dtypes.float8_e5m2, 14)}[fmt]
    v = np.moveaxis(np.asarray(x, np.float32).astype(ml_dtypes.bfloat16).astype(np.float64), axis, -1)
    blocks = v.reshape(v.shape[:-1] + (-1, 32))
    amax = np.abs(blocks).max(-1, keepdims=True)
    byte = np.maximum(np.where(amax > 0, np.frexp(amax)[1] - 1 + 127, 0) - down, 1)
    scale = np.exp2(byte - 127.0)
    codes = (blocks / scale).astype(np.float32).astype(dtype).astype(np.float64)
    return np.moveaxis((codes * scale).reshape(v.shape), -1, axis)


WIDE = False


def mx_kscale(k):
    if not WIDE:
        return np.ones(k)
    levels = np.array([10, -10, 5, -5, 0])
    if k % 512:
        return np.exp2(np.random.permutation(np.resize(levels, k // 32))).repeat(32)
    a = np.empty((k // 512, 16))
    for p in range(k // 512):
        a[p, :8] = np.random.permutation(np.resize(levels, 8))
        for g in range(8):
            far = levels[np.abs(levels - a[p, g]) >= 10]
            a[p, g + 8] = far[np.random.randint(len(far))]
    return np.exp2(a.ravel()).repeat(32)


def f64(x):
    return np.asarray(x).astype(np.float64)


def striped(idx):
    return np.tile(idx.reshape(-1, 16).T, (8, 1)).astype(np.uint16)


def unstriped(offs):
    return offs[:16].T.reshape(-1).astype(np.int64)


E2M1 = np.array([0.0, 0.5, 1.0, 1.5, 2.0, 3.0, 4.0, 6.0, -0.0, -0.5, -1.0, -1.5, -2.0, -3.0, -4.0, -6.0])


def pack_weight(w, fmt):
    k, n = w.shape
    w = f64(np.asarray(w, np.float32).astype(ml_dtypes.bfloat16)).reshape(k // 32, 32, n)
    amax = np.abs(w).max(1)
    if fmt == "e4m3":
        byte = np.frexp(amax)[1] - 1 + 127 - 7
    else:
        mant, ex = np.frexp(amax / 6.0)
        byte = np.where(mant > 0.5, ex, ex - 1) + 127
    byte = np.clip(np.where(amax > 0, byte, 1), 1, 254)
    scaled = (w * np.exp2(127.0 - byte)[:, None, :]).reshape(k, n).astype(np.float32)
    by_word = np.ascontiguousarray(scaled.reshape(k // 512, 128, 4, n).transpose(0, 1, 3, 2))
    if fmt == "e4m3":
        words = by_word.astype(ml_dtypes.float8_e4m3fn).view(np.uint8)
    else:
        c = by_word.astype(ml_dtypes.float4_e2m1fn).view(np.uint8) & 0xF
        words = (c[..., 0::2] | (c[..., 1::2] << 4)).reshape(k // 512, 128, 2 * n)
    return np.ascontiguousarray(words), np.ascontiguousarray(byte.astype(np.uint8).reshape(k // 512, 16, n))


def unpack_weight(words, scales, fmt):
    g, _, n = scales.shape
    words = np.ascontiguousarray(words).reshape(g, 128, n, -1)
    if fmt == "e4m3":
        vals = words.view(ml_dtypes.float8_e4m3fn).astype(np.float64)
    else:
        nib = np.empty((g, 128, n, 4), np.uint8)
        nib[..., 0::2] = words & 0xF
        nib[..., 1::2] = words >> 4
        vals = E2M1[nib]
    vals = vals * np.repeat(np.exp2(scales.astype(np.float64) - 127.0), 8, axis=1)[..., None]
    return vals.transpose(0, 1, 3, 2).reshape(g * 512, n)


def relu(v):
    return np.maximum(v, 0.0)


K, T, E, C, H, N = 2048, 640, 4, 128, 512, 512


def by_expert(wq, xq):
    return np.concatenate([wq[e].T @ xq[:, e * C:(e + 1) * C] for e in range(E)], axis=1)


def setup_inputs():
    n = np.random.standard_normal
    s = mx_kscale(K)[:, None]
    u = mx_kscale(H)
    w1 = [pack_weight(m, "e2m1") for m in n((E, K, H)) / np.sqrt(K) / s[None] * u[None, None, :]]
    w2 = [pack_weight(m, "e2m1") for m in n((E, H, N)) / np.sqrt(H) / u[None, :, None]]
    return {
        "xT": (n((K, T)) * s).astype(np.float32),
        "w1_words": np.stack([m[0] for m in w1]),
        "w1_scales": np.stack([m[1] for m in w1]),
        "w2_words": np.stack([m[0] for m in w2]),
        "w2_scales": np.stack([m[1] for m in w2]),
        "gate": np.tile(np.random.uniform(0.2, 1.0, E * C), (N, 1)).astype(np.float32),
        "offs": striped(np.random.permutation(T)[:E * C]),
    }


def reference(xT, w1_words, w1_scales, w2_words, w2_scales, gate, offs):
    idx = unstriped(offs)
    w1 = np.stack([unpack_weight(w1_words[e], w1_scales[e], "e2m1") for e in range(E)])
    w2 = np.stack([unpack_weight(w2_words[e], w2_scales[e], "e2m1") for e in range(E)])
    xq = mxq(f64(xT)[:, idx], 0, "e4m3")
    h = relu(by_expert(w1, xq))
    y = by_expert(w2, mxq(h, 0, "e4m3"))
    out = np.zeros((N, T))
    out[:, idx] = f64(gate) * y
    return out

from contextlib import ExitStack

import concourse.mybir as mybir
from concourse.masks import make_identity

K, T, E, C, H, N = 2048, 640, 4, 128, 512, 512
SLOTS = E * C
FLOPS = 2 * SLOTS * H * (K + N)

P = 128
PACK = 4
K_PASS = P * PACK
PASSES = K // K_PASS
W = 704
OC = C // 16

F32 = mybir.dt.float32
BF16 = mybir.dt.bfloat16
I32 = mybir.dt.int32
U32 = mybir.dt.uint32
U16 = mybir.dt.uint16
U8 = mybir.dt.uint8
FP8X4 = mybir.dt.float8_e4m3fn_x4
FP4X4 = mybir.dt.float4_e2m1fn_x4
COPY = mybir.ActivationFunctionType.Copy
RELU = mybir.ActivationFunctionType.Relu
MULT = mybir.AluOpType.mult

HALF = T // 2
CHUNKS = {0: ((0, HALF), (HALF, T)), 1: ((0, HALF), (HALF, T)), 2: ((0, HALF), (HALF, T)), 3: ((0, 384), (384, T))}
CASTS = {
    0: ((0, 320, "v"), (320, 480, "s"), (480, 640, "v")),
    1: ((0, 320, "s"), (320, 640, "s")),
    2: ((0, 320, "s"), (320, 640, "s")),
    3: ((0, 256, "s"), (256, 384, "v"), (384, 512, "s"), (512, 640, "v")),
}
QUANTS = {
    0: ((0, 256), (256, 512), (512, 640)),
    1: ((0, 512), (512, 640)),
    2: ((0, 512), (512, 640)),
    3: ((0, 256), (256, 512), (512, 640)),
}


def tile_moe_pln_mlp_relu_kernel(
    tc, xT, w1_words, w1_scales, w2_words, w2_scales, gate, offs, out
):
    nc = tc.nc
    with ExitStack() as ctx:
        keep = ctx.enter_context(tc.tile_pool(name="keep", bufs=1))
        psum_a = ctx.enter_context(tc.psum_pool(name="psum_a", bufs=4))
        psum_t = ctx.enter_context(tc.psum_pool(name="psum_t", bufs=2))
        psum_y = ctx.enter_context(tc.psum_pool(name="psum_y", bufs=2))

        offsets = keep.tile([P, SLOTS // 16], U16, name="offsets")

        raw = [keep.tile([P, PACK, T], F32, name=f"raw{s}") for s in range(PASSES)]
        grouped = [keep.tile([P, T * PACK], BF16, name=f"grouped{s}", align_bytes=64) for s in range(PASSES)]
        words = [keep.tile([P, W], I32, name=f"words{s}", align_bytes=64) for s in range(PASSES)]
        scales = {s: keep.tile([P, W], U8, name=f"scales{s}", align_bytes=64) for s in (0, 2, 3)}
        slot_words = [keep.tile([P, SLOTS], U32, name=f"slot_words{s}", align_bytes=64) for s in range(PASSES)]
        slot_scales = {s: keep.tile([P, SLOTS], U8, name=f"slot_scales{s}", align_bytes=64) for s in (0, 2, 3)}
        shifted = keep.tile([P, SLOTS], U8, name="shifted", align_bytes=64)
        w1w = [keep.tile([P, PASSES, 2 * H], U8, name=f"w1w{e}", align_bytes=64) for e in range(E)]
        w1s_first = keep.tile([P, PASSES, H], U8, name="w1s_first", align_bytes=64)
        w1s_rest = keep.tile([P, (E - 1) * PASSES, H], U8, name="w1s_rest", align_bytes=64)
        w2w = keep.tile([P, E, 2 * N], U8, name="w2w", align_bytes=64)
        w2s = keep.tile([P, E, N], U8, name="w2s", align_bytes=64)
        gates = keep.tile([P, SLOTS], F32, name="gates")
        outs = [keep.tile([P, T], F32, name=f"outs{b}") for b in range(N // P)]
        ident = keep.tile([P, P], F32, name="ident")
        dummy = keep.tile([P, 1], F32, name="dummy")

        for s in range(PASSES):
            for a, b in CHUNKS[s]:
                nc.sync.dma_start(
                    out=raw[s][:, :, a:b],
                    in_=xT[s * K_PASS : (s + 1) * K_PASS, a:b].rearrange("(p j) t -> p j t", j=PACK),
                )
            if s == 0:
                nc.sync.dma_start(offsets[:], offs)

        nc.vector.memset(dummy[:], 0.0)
        nc.scalar.activation(out=dummy[:], in_=dummy[:], func=RELU)
        for s in range(PASSES):
            nc.gpsimd.memset(words[s][:, T:W], 0)
        for s in (0, 2, 3):
            nc.gpsimd.memset(scales[s][:].bitcast(I32), 0)
        nc.gpsimd.memset(shifted[:].bitcast(I32), 0)
        make_identity(nc, ident[:])
        for tile in (w1s_first, w2s, w1s_rest):
            nc.gpsimd.memset(tile[:].rearrange("p s i -> p (s i)").bitcast(I32), 0)
        for b in range(N // P):
            nc.vector.memset(outs[b][:], 0.0)

        def load_w1(e):
            nc.sync.dma_start(out=w1w[e][:].bitcast(I32), in_=w1_words[e].rearrange("s p c -> p s c").bitcast(I32))

        for r in range(4):
            nc.sync.dma_start(
                out=w1s_first[r:P:32, :, :].bitcast(I32),
                in_=w1_scales[0, :, r:16:4, :].rearrange("s q i -> q s i").bitcast(I32),
            )
        load_w1(0)
        for r in range(4):
            nc.sync.dma_start(
                out=w2s[r:P:32, :, :].bitcast(I32),
                in_=w2_scales[:, 0, r:16:4, :].rearrange("e q i -> q e i").bitcast(I32),
            )
        nc.sync.dma_start(out=w2w[:].bitcast(I32), in_=w2_words[:, 0].rearrange("e p c -> p e c").bitcast(I32))
        w1_rows = w1_scales[1:E].rearrange("e s q i -> (e s) q i")
        for r in range(4):
            nc.sync.dma_start(
                out=w1s_rest[r:P:32, :, :].bitcast(I32),
                in_=w1_rows[:, r:16:4, :].rearrange("g q i -> q g i").bitcast(I32),
            )
        load_w1(1)
        nc.sync.dma_start(out=gates[:], in_=gate[0:P, :])
        load_w1(2)
        load_w1(3)

        def cast(s):
            for a, b, eng in CASTS[s]:
                dst = grouped[s][:, a * PACK : b * PACK].rearrange("p (c i t) -> p c t i", i=4, t=PACK)
                src = raw[s][:, :, a:b].rearrange("p t (c i) -> p c t i", i=4)
                if eng == "v":
                    nc.vector.tensor_copy(out=dst, in_=src)
                else:
                    nc.scalar.activation(out=dst, in_=src, func=COPY)

        def quantize(s):
            for a, b in QUANTS[s]:
                nc.vector.quantize_mx(
                    out=words[s][:, a:b].bitcast(FP8X4),
                    scales=scales[0][4:P, a:b] if s == 1 else scales[s][:, a:b],
                    in_=grouped[s][:, a * PACK : b * PACK],
                )

        def gather(s, e0, e1):
            list_part = offsets[:, e0 * OC : e1 * OC]
            nc.vector.tensor_copy(out=slot_words[s][:, e0 * C : e1 * C], in_=words[s][:].bitcast(U32).indirect(list_part))
            if s >= 2:
                gather_scales(s, e0, e1)

        def gather_scales(s, e0, e1):
            list_part = offsets[:, e0 * OC : e1 * OC]
            nc.vector.tensor_copy(out=slot_scales[s][:, e0 * C : e1 * C], in_=scales[s][:].indirect(list_part))

        acc = {}

        def layer1(e, s):
            if s == 0:
                acc[e] = psum_a.tile([P, H], F32, name="a")
            cols = slice(e * C, (e + 1) * C)
            nc.tensor.matmul_mx(
                out=acc[e][:],
                lhsT=slot_words[s][:, cols].bitcast(FP8X4),
                lhsT_scale=shifted[:, cols] if s == 1 else slot_scales[s][:, cols],
                rhs=w1w[e][:, s, :].bitcast(FP4X4),
                rhs_scale=(w1s_first[:, s, :] if e == 0 else w1s_rest[:, (e - 1) * PASSES + s, :]),
                start=(s == 0),
                stop=(s == 3),
            )

        h_rows, h_grouped, h_words, h_scales, y_rows = {}, {}, {}, {}, {}

        def hidden(e):
            h_rows[e] = keep.tile([P, H], BF16, name=f"h_rows{e}")
            nc.scalar.activation(
                out=h_rows[e][:].rearrange("p (u m v) -> p u m v", u=2, v=2),
                in_=acc[e][:].rearrange("p (m u v) -> p u m v", u=2, v=2),
                func=RELU,
            )
            turned = psum_t.tile([P, 2, C], F32, name="turned")
            pairs = h_rows[e][:].bitcast(F32)
            for u in range(2):
                nc.tensor.transpose(turned[:, u, :], pairs[:, u * P : (u + 1) * P], ident[:])
            h_grouped[e] = keep.tile([P, C * PACK], BF16, name=f"h_grouped{e}", align_bytes=64)
            nc.scalar.copy(
                out=h_grouped[e][:].bitcast(F32).rearrange("p (c u) -> p c u", u=2),
                in_=turned[:].rearrange("p u c -> p c u"),
            )

        def hidden_quantize(e):
            h_words[e] = keep.tile([P, C], U32, name=f"h_words{e}", align_bytes=64)
            h_scales[e] = keep.tile([P, C], U8, name=f"h_scales{e}", align_bytes=64)
            nc.vector.quantize_mx(out=h_words[e][:].bitcast(FP8X4), scales=h_scales[e][:], in_=h_grouped[e][:])

        def layer2(e):
            y = psum_y.tile([P, N // P, C], F32, name="y")
            for b in range(N // P):
                nc.tensor.matmul_mx(
                    out=y[:, b, :],
                    lhsT=w2w[:, e, b * 2 * P : (b + 1) * 2 * P].bitcast(FP4X4),
                    lhsT_scale=w2s[:, e, b * P : (b + 1) * P],
                    rhs=h_words[e][:].bitcast(FP8X4),
                    rhs_scale=h_scales[e][:],
                    start=True,
                    stop=True,
                )
            return y

        y_first = [keep.tile([P, N // P, C], F32, name=f"y_first{e}") for e in range(2)]
        y_last = keep.tile([P, N // P, 2 * C], F32, name="y_last")

        def leave(e, y):
            if e < 2:
                nc.scalar.activation(out=y_first[e][:], in_=y[:], func=COPY)
            else:
                nc.scalar.activation(out=y_last[:, :, (e - 2) * C : (e - 1) * C], in_=y[:], func=COPY)

        def scatter(b, e0, e1, y):
            nc.vector.tensor_tensor(
                outs[b][:].indirect(offsets[:, e0 * OC : e1 * OC]), y, gates[:, e0 * C : e1 * C], MULT
            )

        for s in range(2):
            cast(s)
            quantize(s)
            gather(s, 0, E)
        gather_scales(0, 0, E)
        cast(2)
        nc.scalar.dma_start(out=shifted[0:100, :].bitcast(I32), in_=slot_scales[0][4:104, :].bitcast(I32))
        quantize(2)
        gather(2, 0, 1)
        cast(3)
        quantize(3)
        gather(3, 0, 1)
        for s in range(PASSES):
            layer1(0, s)
        hidden(0)
        gather(2, 1, 2)
        gather(3, 1, 2)
        for s in range(PASSES):
            layer1(1, s)
        hidden(1)
        gather(2, 2, 4)
        for e in (2, 3):
            for s in range(2):
                layer1(e, s)
        hidden_quantize(0)
        leave(0, layer2(0))
        gather(3, 2, 4)
        hidden_quantize(1)
        leave(1, layer2(1))
        for e in (2, 3):
            for s in (2, 3):
                layer1(e, s)
            hidden(e)
        for b in range(N // P):
            scatter(b, 0, 1, y_first[0][:, b, :])
        hidden_quantize(2)
        hidden_quantize(3)
        leave(2, layer2(2))
        leave(3, layer2(3))
        for b in range(N // P):
            scatter(b, 1, 2, y_first[1][:, b, :])
        for b in range(N // P):
            scatter(b, 2, 4, y_last[:, b, :])
            nc.sync.dma_start(out=out[b * P : (b + 1) * P, :], in_=outs[b][:])
